import numpy as np, ml_dtypes
CORES = [1,14,19,24,37,42,55,60,65,78,83,88,101,106,119,124]
N = 16
NP, NBK, TK, CAP = 8, 4, 128, 10
DEST = [[10,8,9,12],[14,10,8,8],[8,13,10,15],[8,10,8,14],[8,9,13,10],[8,15,15,11],[9,13,8,11],[8,12,13,10]]
def setup_inputs(rng):
    return {"x": rng.standard_normal((N, 128, NBK * TK), dtype=np.float32).astype(ml_dtypes.bfloat16), "w": (rng.standard_normal((N, 128, 128), dtype=np.float32) / 8).astype(ml_dtypes.bfloat16)}
def setup_inputs_big(rng):
    d = setup_inputs(rng)
    for k in ("x", "w"): d[k] = (d[k].astype(np.float32) * 1024.0).astype(d[k].dtype)
    return d
def setup_inputs_small(rng):
    d = setup_inputs(rng)
    for k in ("x", "w"): d[k] = (d[k].astype(np.float32) * (1 / 1024.0)).astype(d[k].dtype)
    return d
def reference(x, w):
    X, W = x.astype(np.float64), w.astype(np.float64)
    y = np.full((N, 128, CAP * TK), np.nan); n = [0] * N
    for p in range(NP):
        for c in range(NBK):
            q = DEST[p][c]
            y[q][:, TK * n[q]:TK * n[q] + TK] = W[q].T @ np.maximum(W[p].T @ X[p][:, TK * c:TK * c + TK], 0.0)
            n[q] += 1
    return {"y": y.astype(ml_dtypes.bfloat16 if x.dtype != np.float64 else np.float64)}

from concourse.mybir import AluOpType

NSIM = 128
TK = 128
NPS = 8
ENG = 4
RELAY = "A"
S_OWN = 1
S_H1 = 1
S_FW = 1
WIDE = True

SCRATCH = {
    "wsb": ("sbuf", [128, 128], "bfloat16"),
    "xsb": ("sbuf", [128, 512], "bfloat16"),
    "hsb": ("sbuf", [128, 512], "bfloat16"),
    "zero": ("sbuf", [128, 512], "float32"),
    "land": ("sbuf", [128, 1280], "bfloat16"),
    "ysb": ("sbuf", [128, 1280], "bfloat16"),
}
for _k in range(NPS):
    SCRATCH["ps%d" % _k] = ("psum", [128, 512], "float32")

SEMAPHORES = (["wl", "xl", "zs", "sent", "st"] + ["m%d" % k for k in range(NPS)] + ["c%d" % k for k in range(NPS)]
              + ["a%d_%d" % (p, k) for p in range(8) for k in range(4)])


def _bits(mask):
    return [b for b in range(mask.bit_length()) if (mask >> b) & 1]


def _engine_sets(src, topo):
    near = [c for c in range(NSIM) if c != src and topo.chip(c) == topo.chip(src)][0]
    far = [c for c in range(NSIM) if topo.chip(c) != topo.chip(src) and topo.may_write(src, c)][0]
    lo = _bits(topo.mask(src, far))
    hi = [b for b in _bits(topo.mask(src, near)) if b not in lo]
    sets = []
    for grp in (hi, lo):
        k = len(grp) // ENG
        for i in range(k):
            sets.append(grp[i::k])
    return sets


def _plan(T, topo):
    cores = list(T.cores)
    dest = T.tables["DEST"]
    npr = len(dest)
    owned = {}
    pieces = []
    for p, row in enumerate(dest):
        mine = {}
        for c, q in enumerate(row):
            s = owned.get(q, 0)
            owned[q] = s + 1
            if q not in mine:
                mine[q] = []
                pieces.append(mine[q])
            mine[q].append((p, c, q, s))

    sets, load = {}, {}

    def pick(src, dst, k, nb):
        if src not in sets:
            sets[src] = _engine_sets(src, topo)
            load[src] = [0] * len(sets[src])
        ok = set(_bits(topo.mask(src, dst)))
        cand = [i for i, s in enumerate(sets[src]) if set(s) <= ok]
        cand.sort(key=lambda j: (load[src][j], j))
        use = cand[:k * (min(nb, 2) if WIDE else 1)]
        mask = 0
        for i in use:
            load[src][i] += nb / len(use)
            mask |= sum(1 << b for b in sets[src][i])
        return mask

    def one_hop(pc):
        return topo.may_write(cores[pc[0][0]], cores[pc[0][2]])

    port = {}
    for pc in pieces:
        if one_hop(pc):
            key = (pc[0][2], topo.die(cores[pc[0][0]]))
            port[key] = port.get(key, 0) + len(pc)

    two = [pc for pc in pieces if not one_hop(pc)]
    via = {}
    if RELAY == "A":
        taken = set(cores)
        for pc in sorted(two, key=lambda pc: (-owned[pc[0][2]], pc[0][0])):
            src, dst = cores[pc[0][0]], cores[pc[0][2]]
            cand = [c for c in range(NSIM) if topo.chip(c) == topo.chip(src) and c not in taken
                    and topo.may_write(c, dst)]
            v = min(cand, key=lambda c: (topo.die(c) != topo.die(src), c))
            taken.add(v)
            via[(pc[0][0], pc[0][2])] = v
    else:
        groups = {}
        for pc in two:
            src, dst = cores[pc[0][0]], cores[pc[0][2]]
            cand = tuple(c for c in cores[:npr] if c != src and topo.may_write(src, c) and topo.may_write(c, dst))
            groups.setdefault((cand, pc[0][2]), []).append(pc)
        work = {}
        for (cand, q), pcs in sorted(groups.items(), key=lambda kv: (-sum(len(pc) for pc in kv[1]), kv[0][1])):
            v = min(cand, key=lambda c: (work.get(c, 0), port.get((q, topo.die(c)), 0), c))
            nb = sum(len(pc) for pc in pcs)
            work[v] = work.get(v, 0) + nb
            port[(q, topo.die(v))] = port.get((q, topo.die(v)), 0) + nb
            for pc in pcs:
                via[(pc[0][0], q)] = v

    first = {}
    for v in sorted(set(via.values())):
        srcs = sorted({p for (p, q), c in via.items() if c == v})
        qs = {p: [q for (pp, q), c in sorted(via.items()) if c == v and pp == p] for p in srcs}
        head = {}
        for a, b in zip(srcs, srcs[1:]):
            shared = [q for q in qs[a] if q in qs[b] and (head.get(a) != q or len(qs[a]) == 1)]
            if shared:
                q = max(shared, key=lambda q: owned[q])
                qs[a] = [x for x in qs[a] if x != q] + [q]
                qs[b] = [q] + [x for x in qs[b] if x != q]
                head[b] = q
        for p in srcs:
            first[(p, v)] = [[pc for pc in two if pc[0][0] == p and pc[0][2] == q][0] for q in qs[p]]

    own = {p: [] for p in range(npr)}
    for (p, v), pcs in first.items():
        own[p].append({"src": cores[p], "dst": v, "blocks": [b for pc in pcs for b in pc], "hops": 2, "needs": []})
    for p in range(npr):
        own[p].sort(key=lambda w: (-max(owned[b[2]] for b in w["blocks"]), w["dst"]))
        rest = [pc for pc in pieces if pc[0][0] == p and one_hop(pc)]
        for pc in sorted(rest, key=lambda pc: -owned[pc[0][2]]):
            own[p].append({"src": cores[p], "dst": cores[pc[0][2]], "blocks": list(pc), "hops": 1, "needs": []})
        col = 0
        for i, w in enumerate(own[p]):
            w["i"], w["scol"] = i, col
            col += TK * len(w["blocks"])
            w["mask"] = pick(w["src"], w["dst"], S_H1 if w["hops"] == 2 else S_OWN, len(w["blocks"]))

    fwd = {}
    for v in sorted(set(via.values())):
        seq = []
        for p in sorted({p for (p, vv) in first if vv == v}):
            w = [w for w in own[p] if w["dst"] == v][0]
            w["dcol"] = TK * len(seq)
            seq += [(b, w) for b in w["blocks"]]
        fwd[v] = []
        for j, (b, w) in enumerate(seq):
            if fwd[v] and fwd[v][-1]["blocks"][-1][2] == b[2]:
                f = fwd[v][-1]
                f["blocks"].append(b)
                if w not in f["needs"]:
                    f["needs"].append(w)
            else:
                fwd[v].append({"src": v, "dst": cores[b[2]], "blocks": [b], "hops": 2, "needs": [w], "scol": TK * j})
        fwd[v].sort(key=lambda f: (max(w["i"] for w in f["needs"]), -len(f["blocks"])))
        for i, f in enumerate(fwd[v]):
            f["i"] = 10 + i + max(w["i"] for w in f["needs"])
            f["mask"] = pick(v, f["dst"], S_FW, len(f["blocks"]))

    inq = {}
    for w in [w for p in range(npr) for w in own[p] if w["hops"] == 1] + [f for v in sorted(fwd) for f in fwd[v]]:
        inq.setdefault(w["dst"], []).append(w)
    for ws in inq.values():
        ws.sort(key=lambda w: (w["i"], len(w["blocks"]), w["blocks"][0][0]))
        col = 0
        for w in ws:
            w["dcol"] = col
            col += TK * len(w["blocks"])
    for ws in list(own.values()) + list(fwd.values()):
        for w in ws:
            w["sem"] = "a%d_%d" % (w["blocks"][0][0], w["blocks"][0][1])
            w["n"] = TK * len(w["blocks"])
            w["eng"] = len(_bits(w["mask"]))
    return own, fwd, inq


def _send(g, T, topo, w, buf):
    rid, pid, _ = topo.addr(w["dst"])
    g.remote_dma(out_ap=T.land[:, w["dcol"]:w["dcol"] + w["n"]], in_ap=buf[:, w["scol"]:w["scol"] + w["n"]],
                 remote_sem=T.sem[w["sem"]], local_sem=T.sem.sent, pid=pid, routing_id=rid,
                 dma_engine_mask=w["mask"])
    return w["eng"]


def _pass_on(g, T, topo, todo):
    total = 0
    seen = []
    for f in todo:
        for w in f["needs"]:
            if w["sem"] not in seen:
                seen.append(w["sem"])
                g.wait_ge(T.sem[w["sem"]], w["eng"])
        total += _send(g, T, topo, f, T.land)
    return total


def rank_program(g, core, T, topo):
    own, fwd, inq = _plan(T, topo)
    rank = T.rank_of(core)

    if rank is None:
        if core in fwd:
            g.wait_ge(T.sem.sent, _pass_on(g, T, topo, fwd[core]))
        return

    if rank in own:
        g.scalar.dma_start(T.wsb[:], T.w[:]).then_inc(T.sem.wl, 16)
        g.sync.dma_start(T.xsb[:], T.x[:]).then_inc(T.sem.xl, 16)
        g.vector.memset(T.zero[:], 0.0).then_inc(T.sem.zs, 1)
        g.tensor.wait_ge(T.sem.wl, 16)
        g.tensor.wait_ge(T.sem.xl, 16)
        g.vector.wait_ge(T.sem.zs, 1)
        total = 0
        for k, w in enumerate(own[rank]):
            n, off = w["n"], w["scol"]
            ps = T["ps%d" % k]
            for j, b in enumerate(w["blocks"]):
                g.tensor.matmul(ps[:, TK * j:TK * j + TK], T.wsb[:], T.xsb[:, TK * b[1]:TK * b[1] + TK], True,
                                True).then_inc(T.sem["m%d" % k], 1)
            g.vector.wait_ge(T.sem["m%d" % k], len(w["blocks"]))
            g.vector.tensor_tensor(T.hsb[:, off:off + n], ps[:, 0:n], T.zero[:, 0:n],
                                   AluOpType.max).then_inc(T.sem["c%d" % k], 1)
            g.wait_ge(T.sem["c%d" % k], 1)
            total += _send(g, T, topo, w, T.hsb)
        total += _pass_on(g, T, topo, fwd.get(core, []))
        g.wait_ge(T.sem.sent, total)
        return

    g.sync.dma_start(T.wsb[:], T.w[:]).then_inc(T.sem.wl, 16)
    g.tensor.wait_ge(T.sem.wl, 16)
    stores = 0
    for k, w in enumerate(inq.get(core, [])):
        a, n = w["dcol"], w["n"]
        ps = T["ps%d" % k]
        g.tensor.wait_ge(T.sem[w["sem"]], w["eng"])
        g.tensor.matmul(ps[:, 0:n], T.wsb[:], T.land[:, a:a + n], True, True).then_inc(T.sem["m%d" % k], 1)
        g.vector.wait_ge(T.sem["m%d" % k], 1)
        g.vector.tensor_copy(T.ysb[:, a:a + n], ps[:, 0:n]).then_inc(T.sem["c%d" % k], 1)
        runs = []
        for j, b in enumerate(w["blocks"]):
            if runs and runs[-1][1] + runs[-1][2] == b[3]:
                runs[-1][2] += 1
            else:
                runs.append([j, b[3], 1])
        for j, slot, nb in runs:
            dq = g.sync if stores % 2 == 0 else g.scalar
            stores += 1
            dq.wait_ge(T.sem["c%d" % k], 1)
            dq.dma_start(T.y[:, TK * slot:TK * (slot + nb)],
                         T.ysb[:, a + TK * j:a + TK * (j + nb)]).then_inc(T.sem.st, 16)
    g.wait_ge(T.sem.st, 16 * stores)
